import numpy as np
import ml_dtypes


def mxq(x, axis, fmt="e4m3"):
    dtype, down = {"e4m3": (ml_dtypes.float8_e4m3fn, 7), "e5m2": (ml_dtypes.float8_e5m2, 14)}[fmt]
    v = np.moveaxis(np.asarray(x, np.float32).astype(ml_dtypes.bfloat16).astype(np.float64), axis, -1)
    blocks = v.reshape(v.shape[:-1] + (-1, 32))
    amax = np.abs(blocks).max(-1, keepdims=True)
    byte = np.maximum(np.where(amax > 0, np.frexp(amax)[1] - 1 + 127, 0) - down, 1)
    scale = np.exp2(byte - 127.0)
    codes = (blocks / scale).astype(np.float32).astype(dtype).astype(np.float64)
    return np.moveaxis((codes * scale).reshape(v.shape), -1, axis)


WIDE = False


def mx_kscale(k):
    if not WIDE:
        return np.ones(k)
    levels = np.array([10, -10, 5, -5, 0])
    if k % 512:
        return np.exp2(np.random.permutation(np.resize(levels, k // 32))).repeat(32)
    a = np.empty((k // 512, 16))
    for p in range(k // 512):
        a[p, :8] = np.random.permutation(np.resize(levels, 8))
        for g in range(8):
            far = levels[np.abs(levels - a[p, g]) >= 10]
            a[p, g + 8] = far[np.random.randint(len(far))]
    return np.exp2(a.ravel()).repeat(32)


def f64(x):
    return np.asarray(x).astype(np.float64)


def striped(idx):
    return np.tile(np.asarray(idx).reshape(-1, 16).T, (8, 1)).astype(np.uint16)


def unstriped(offs):
    return offs[:16].T.reshape(-1).astype(np.int64)


def striped8(idx):
    return np.asarray(idx).reshape(8, -1, 16).transpose(0, 2, 1).reshape(128, -1).astype(np.uint16)


def unstriped8(offs):
    return offs.reshape(8, 16, -1).transpose(0, 2, 1).reshape(8, -1).astype(np.int64)


def pick8(x, idx, run):
    r = np.arange(len(x))
    return x[r[:, None], idx[r % (8 * run) // run]]


E2M1 = np.array([0.0, 0.5, 1.0, 1.5, 2.0, 3.0, 4.0, 6.0, -0.0, -0.5, -1.0, -1.5, -2.0, -3.0, -4.0, -6.0])


def pack_weight(w, fmt):
    k, n = w.shape
    w = f64(np.asarray(w, np.float32).astype(ml_dtypes.bfloat16)).reshape(k // 32, 32, n)
    amax = np.abs(w).max(1)
    if fmt == "e4m3":
        byte = np.frexp(amax)[1] - 1 + 127 - 7
    else:
        mant, ex = np.frexp(amax / 6.0)
        byte = np.where(mant > 0.5, ex, ex - 1) + 127
    byte = np.clip(np.where(amax > 0, byte, 1), 1, 254)
    scaled = (w * np.exp2(127.0 - byte)[:, None, :]).reshape(k, n).astype(np.float32)
    by_word = np.ascontiguousarray(scaled.reshape(k // 512, 128, 4, n).transpose(0, 1, 3, 2))
    if fmt == "e4m3":
        words = by_word.astype(ml_dtypes.float8_e4m3fn).view(np.uint8)
    else:
        c = by_word.astype(ml_dtypes.float4_e2m1fn).view(np.uint8) & 0xF
        words = (c[..., 0::2] | (c[..., 1::2] << 4)).reshape(k // 512, 128, 2 * n)
    return np.ascontiguousarray(words), np.ascontiguousarray(byte.astype(np.uint8).reshape(k // 512, 16, n))


def unpack_weight(words, scales, fmt):
    g, _, n = scales.shape
    words = np.ascontiguousarray(words).reshape(g, 128, n, -1)
    if fmt == "e4m3":
        vals = words.view(ml_dtypes.float8_e4m3fn).astype(np.float64)
    else:
        nib = np.empty((g, 128, n, 4), np.uint8)
        nib[..., 0::2] = words & 0xF
        nib[..., 1::2] = words >> 4
        vals = E2M1[nib]
    vals = vals * np.repeat(np.exp2(scales.astype(np.float64) - 127.0), 8, axis=1)[..., None]
    return vals.transpose(0, 1, 3, 2).reshape(g * 512, n)


K, J, R, T, C, S, N, Z, U, E = 512, 384, 512, 1024, 512, 128, 256, 1024, 1024, 256


def setup_inputs():
    n = np.random.standard_normal
    idx = np.random.permutation(T)[:J]
    idx2 = np.stack([np.random.permutation(C)[:J] for _ in range(8)])
    idx3 = np.stack([np.random.permutation(C)[:J] for _ in range(8)])
    idx4 = np.stack([np.random.permutation(C)[:S] for _ in range(8)])
    idx5 = np.stack([np.random.permutation(C)[:S] for _ in range(8)])
    idx6 = np.random.permutation(Z)[:N]
    idx7 = np.stack([np.random.permutation(U)[:C] for _ in range(8)])
    fk = mx_kscale(K)
    fr = mx_kscale(R)
    xtp = pack_weight(n((K, T)) * fk[:, None], "e2m1")
    wp = pack_weight(n((K, R)) * 1 / np.sqrt(K) / fk[:, None] * fr, "e4m3")
    w2p = pack_weight(n((K, R)) * 1 / np.sqrt(K) / fk[:, None] * fr, "e4m3")
    vsp = pack_weight(n((R, Z)) * 1 / np.sqrt(R) / fr[:, None], "e4m3")
    return {
        "xt_words": xtp[0],
        "xt_scales": xtp[1],
        "w_words": wp[0],
        "w_scales": wp[1],
        "w2_words": w2p[0],
        "w2_scales": w2p[1],
        "sa": (np.random.uniform(0.5, 1.6, (R, 1))).astype(np.float32),
        "vs_words": vsp[0],
        "vs_scales": vsp[1],
        "offs": striped(idx),
        "offs2": striped8(idx2),
        "offs3": striped8(idx3),
        "offs4": striped8(idx4),
        "offs5": striped8(idx5),
        "offs6": striped(idx6),
        "offs7": striped8(idx7),
    }


def reference(xt_words, xt_scales, w_words, w_scales, w2_words, w2_scales, sa, vs_words, vs_scales, offs, offs2, offs3, offs4, offs5, offs6, offs7):
    idx = unstriped(offs)
    idx2 = unstriped8(offs2)
    idx3 = unstriped8(offs3)
    idx4 = unstriped8(offs4)
    idx5 = unstriped8(offs5)
    idx6 = unstriped(offs6)
    idx7 = unstriped8(offs7)
    xtu = unpack_weight(xt_words, xt_scales, "e2m1")
    wu = unpack_weight(w_words, w_scales, "e4m3")
    w2u = unpack_weight(w2_words, w2_scales, "e4m3")
    vsu = unpack_weight(vs_words, vs_scales, "e4m3")
    xtidxg = xtu[:, idx]
    a = wu.T @ xtidxg
    b = w2u.T @ xtidxg
    pw = np.zeros((R, C))
    pw[np.arange(R)[:, None], idx2[np.arange(R) % 512 // 64]] = a
    pv = np.zeros((R, C))
    pv[np.arange(R)[:, None], idx3[np.arange(R) % 512 // 64]] = b
    h1 = pick8(pw, idx4, 64) * f64(sa)
    pu = np.zeros((R, C))
    pu[np.arange(R)[:, None], idx5[np.arange(R) % 512 // 64]] = h1
    hid = np.abs(pv - pu)
    vsidx6g = vsu[:, idx6]
    hidq = mxq(hid, 0, "e4m3")
    p = vsidx6g.T @ hidq
    m0 = np.zeros((N, U))
    m0[np.arange(N)[:, None], idx7[np.arange(N) % 128 // 16]] = p
    m1 = m0.reshape(N, E, U // E).mean(axis=2)
    m2 = np.repeat(m1, U // E, axis=1)
    y = m0 - m2
    return y

@@ -1,0 +1,228 @@
+from contextlib import ExitStack
+
+import concourse.mybir as mybir
+
+F32 = mybir.dt.float32
+BF16 = mybir.dt.bfloat16
+I32 = mybir.dt.int32
+U32 = mybir.dt.uint32
+U16 = mybir.dt.uint16
+U8 = mybir.dt.uint8
+FP8X4 = mybir.dt.float8_e4m3fn_x4
+FP4X4 = mybir.dt.float4_e2m1fn_x4
+ALU = mybir.AluOpType
+COPY = mybir.ActivationFunctionType.Copy
+AXIS_X = mybir.AxisListType.X
+
+K, J, R, T, C, S, N, Z, U, E = 512, 384, 512, 1024, 512, 128, 256, 1024, 1024, 256
+FLOPS = 2 * (2 * K * R * J + R * N * C)
+
+P = 128
+PACK = 4
+QUADS = 4
+LANES = 16
+BUCKET = U // E
+SLOT_PIECES = ((0, 128), (128, 384))
+COLUMN_PIECES = ((0, 128), (128, 256), (256, 512))
+LAST_PIECES = 4
+
+
+def entries(offsets, lo, hi):
+    return offsets[:, lo // LANES : hi // LANES]
+
+
+def tile_picked_tokens_plain_twin_reposted_store_endcontrast_kernel(
+    tc, xt_words, xt_scales, w_words, w_scales, w2_words, w2_scales, sa, vs_words, vs_scales,
+    offs, offs2, offs3, offs4, offs5, offs6, offs7, out,
+):
+    nc = tc.nc
+    with ExitStack() as ctx:
+        keep = ctx.enter_context(tc.tile_pool(name="keep", bufs=1))
+        psum = ctx.enter_context(tc.psum_pool(name="psum", bufs=8))
+
+        def load_list(name, src):
+            tile = keep.tile(list(src.shape), U16, name=name)
+            nc.sync.dma_start(tile[:], src)
+            return tile
+
+        def load_words(name, src_i32, dtype, columns):
+            tile = keep.tile([P, columns], dtype, name=name, align_bytes=64)
+            nc.sync.dma_start(tile[:].bitcast(I32), src_i32)
+            return tile
+
+        def load_scale_rows(name, src):
+            width = src.shape[2] // 4
+            rows = keep.tile([PACK, QUADS, width], I32, name=name)
+            nc.sync.dma_start(rows[:], src[0].bitcast(I32).rearrange("(q i) c -> i q c", i=PACK))
+            return rows
+
+        def spread_scale_rows(name, rows):
+            width = rows[:].shape[2]
+            plane = keep.tile([P, 4 * width], U8, name=name, align_bytes=64)
+            view = plane[:].bitcast(I32)
+            nc.vector.memset(view, 0)
+            for q in range(QUADS):
+                nc.vector.tensor_copy(view[32 * q : 32 * q + PACK, :], rows[:, q, :])
+            return plane
+
+        def fp8_words(src):
+            return src[0].rearrange("p n t -> p (n t)").bitcast(I32)
+
+        def board(name, columns):
+            tile = keep.tile([P, columns], F32, name=name)
+            nc.vector.memset(tile[:], 0.0)
+            return tile
+
+        xt_rows = load_scale_rows("xt_rows", xt_scales)
+        list1 = load_list("list1", offs)
+        xt_table = load_words("xt_table", xt_words[0].bitcast(I32), U16, T)
+        w_rows = load_scale_rows("w_rows", w_scales)
+        w_raw = load_words("w_raw", fp8_words(w_words), I32, R)
+        list2 = load_list("list2", offs2)
+        w2_rows = load_scale_rows("w2_rows", w2_scales)
+        w2_raw = load_words("w2_raw", fp8_words(w2_words), I32, R)
+        list3 = load_list("list3", offs3)
+        list4 = load_list("list4", offs4)
+        gain = keep.tile([P, PACK], F32, name="gain")
+        nc.sync.dma_start(gain[:], sa.rearrange("(p t) o -> p (t o)", t=PACK))
+        list5 = load_list("list5", offs5)
+        list6 = load_list("list6", offs6)
+        vs_rows = load_scale_rows("vs_rows", vs_scales)
+        vs_table = load_words("vs_table", fp8_words(vs_words), U32, Z)
+        list7 = load_list("list7", offs7)
+
+        xt_plane = spread_scale_rows("xt_plane", xt_rows)
+        token_words, token_scales = [], []
+
+        def gather_tokens(i):
+            lo, hi = SLOT_PIECES[i]
+            words = keep.tile([P, hi - lo], U16, name="token_words%d" % i, align_bytes=64)
+            scales = keep.tile([P, hi - lo], U8, name="token_scales%d" % i, align_bytes=64)
+            nc.vector.tensor_copy(scales[:], xt_plane[:].indirect(entries(list1, lo, hi)))
+            nc.vector.tensor_copy(words[:], xt_table[:].indirect(entries(list1, lo, hi)))
+            token_words.append(words)
+            token_scales.append(scales)
+
+        def deal(name, raw, plane, t):
+            words = keep.tile([P, P], I32, name="%s_words%d" % (name, t), align_bytes=64)
+            scales = keep.tile([P, P], U8, name="%s_scales%d" % (name, t), align_bytes=64)
+            nc.vector.tensor_copy(scales[:], plane[:, t::PACK])
+            nc.vector.tensor_copy(words[:], raw[:, t::PACK])
+            return words, scales
+
+        def multiply_tokens(acc, weights, i):
+            nc.tensor.matmul_mx(
+                out=acc, lhsT=weights[0][:].bitcast(FP8X4), lhsT_scale=weights[1][:],
+                rhs=token_words[i][:].bitcast(FP4X4), rhs_scale=token_scales[i][:], start=True, stop=True,
+            )
+
+        def product(name, weights):
+            acc = psum.tile([P, 512], F32, name="bank")
+            for i, (lo, hi) in enumerate(SLOT_PIECES):
+                multiply_tokens(acc[:, lo:hi], weights, i)
+            result = keep.tile([P, J], F32, name=name)
+            nc.vector.tensor_copy(result[:], acc[:, 0:J])
+            return result
+
+        pw = [board("pw0", C)]
+        gather_tokens(0)
+        w_plane = spread_scale_rows("w_plane", w_rows)
+        first_weights = deal("w", w_raw, w_plane, 0)
+        first = keep.tile([P, J], F32, name="a0")
+        for i, (lo, hi) in enumerate(SLOT_PIECES):
+            if i > 0:
+                gather_tokens(i)
+            acc = psum.tile([P, 512], F32, name="bank")
+            multiply_tokens(acc[:, 0 : hi - lo], first_weights, i)
+            nc.vector.tensor_copy(first[:, lo:hi], acc[:, 0 : hi - lo])
+        w2_plane = spread_scale_rows("w2_plane", w2_rows)
+        a, b, pv, pu = [first], [], [], []
+        for t in range(PACK):
+            if t > 0:
+                pw.append(board("pw%d" % t, C))
+                a.append(product("a%d" % t, deal("w", w_raw, w_plane, t)))
+            pv.append(board("pv%d" % t, C))
+            b.append(product("b%d" % t, deal("w2", w2_raw, w2_plane, t)))
+            pu.append(board("pu%d" % t, C))
+
+        vs_plane = spread_scale_rows("vs_plane", vs_rows)
+        store_words = keep.tile([P, N], U32, name="store_words", align_bytes=64)
+        store_scales = keep.tile([P, N], U8, name="store_scales", align_bytes=64)
+        nc.vector.tensor_copy(store_scales[:], vs_plane[:].indirect(list6[:]))
+        nc.vector.tensor_copy(store_words[:], vs_table[:].indirect(list6[:]))
+        pages = [board("page%d" % nt, U) for nt in range(N // P)]
+
+        def scatter(window, offsets, values):
+            nc.scalar.activation(window[:].indirect(offsets), values, COPY)
+
+        picked = [keep.tile([P, S], F32, name="picked%d" % t) for t in range(PACK)]
+
+        def pick(t):
+            nc.scalar.activation(picked[t][:], pw[t][:].indirect(list4[:]), COPY, scale=gain[:, t : t + 1])
+
+        for lo, hi in SLOT_PIECES:
+            scatter(pw[0], entries(list2, lo, hi), a[0][:, lo:hi])
+        for t in range(PACK):
+            if t + 1 < PACK:
+                scatter(pv[t], list3[:], b[t][:])
+                pick(t)
+                scatter(pw[t + 1], list2[:], a[t + 1][:])
+            else:
+                pick(t)
+                scatter(pv[t], list3[:], b[t][:])
+            scatter(pu[t], list5[:], picked[t][:])
+
+        hid = keep.tile([P, C, PACK], BF16, name="hid", align_bytes=64)
+        diff = [keep.tile([P, C], F32, name="diff%d" % t) for t in range(PACK)]
+
+        def contrast(t, lo, hi):
+            nc.vector.tensor_tensor(diff[t][:, lo:hi], pv[t][:, lo:hi], pu[t][:, lo:hi], ALU.subtract)
+            nc.vector.scalar_tensor_tensor(
+                hid[:, lo:hi, t], diff[t][:, lo:hi], -1.0, diff[t][:, lo:hi], ALU.mult, ALU.max
+            )
+
+        for t in range(PACK - 1):
+            contrast(t, 0, C)
+
+        results = [keep.tile([P, C], F32, name="result%d" % nt) for nt in range(N // P)]
+        for i, (lo, hi) in enumerate(COLUMN_PIECES):
+            contrast(PACK - 1, lo, hi)
+            codes = keep.tile([P, hi - lo], U32, name="hid_words%d" % i, align_bytes=64)
+            scales = keep.tile([P, hi - lo], U8, name="hid_scales%d" % i, align_bytes=64)
+            nc.vector.quantize_mx(
+                out=codes[:].bitcast(FP8X4), scales=scales[:],
+                in_=hid[:, lo:hi, :].rearrange("p c t -> p (c t)"),
+            )
+            for nt in range(N // P):
+                acc = psum.tile([P, 512], F32, name="bank")
+                nc.tensor.matmul_mx(
+                    out=acc[:, 0 : hi - lo],
+                    lhsT=store_words[:, nt * P : (nt + 1) * P].bitcast(FP8X4),
+                    lhsT_scale=store_scales[:, nt * P : (nt + 1) * P],
+                    rhs=codes[:].bitcast(FP8X4), rhs_scale=scales[:], start=True, stop=True,
+                )
+                nc.vector.tensor_copy(results[nt][:, lo:hi], acc[:, 0 : hi - lo])
+
+        def post(nt, lo, hi):
+            scatter(pages[nt], entries(list7, lo, hi), results[nt][:, lo:hi])
+
+        post(0, *COLUMN_PIECES[0])
+        post(1, *COLUMN_PIECES[0])
+        for lo, hi in COLUMN_PIECES[1:]:
+            post(0, lo, hi)
+        post(1, COLUMN_PIECES[1][0], C)
+
+        for nt in range(N // P):
+            width = U // LAST_PIECES
+            sums = keep.tile([P, E], F32, name="sums%d" % nt)
+            final = keep.tile([P, U], F32, name="final%d" % nt)
+            for lo in range(0, U, width):
+                page = pages[nt][:, lo : lo + width].rearrange("p (e j) -> p e j", j=BUCKET)
+                total = sums[:, lo // BUCKET : (lo + width) // BUCKET]
+                nc.vector.tensor_reduce(total, page, AXIS_X, ALU.add)
+                nc.vector.scalar_tensor_tensor(
+                    final[:, lo : lo + width].rearrange("p (e j) -> p e j", j=BUCKET),
+                    total.unsqueeze(2).to_broadcast([P, width // BUCKET, BUCKET]),
+                    -1.0 / BUCKET, page, ALU.mult, ALU.add,
+                )
+                nc.sync.dma_start(out[nt * P : (nt + 1) * P, lo : lo + width], final[:, lo : lo + width])

@@ -12,6 +12,7 @@ FP8X4 = mybir.dt.float8_e4m3fn_x4
 FP4X4 = mybir.dt.float4_e2m1fn_x4
 ALU = mybir.AluOpType
 COPY = mybir.ActivationFunctionType.Copy
+ABS = mybir.ActivationFunctionType.Abs
 AXIS_X = mybir.AxisListType.X
 
 K, J, R, T, C, S, N, Z, U, E = 512, 384, 512, 1024, 512, 128, 256, 1024, 1024, 256
@@ -22,8 +23,10 @@ PACK = 4
 QUADS = 4
 LANES = 16
 BUCKET = U // E
-SLOT_PIECES = ((0, 128), (128, 384))
-COLUMN_PIECES = ((0, 128), (128, 256), (256, 512))
+HEAD = 128
+EARLY = 2
+SLOT_PIECES = ((0, HEAD), (HEAD, J))
+COLUMN_PIECES = ((0, 64), (64, 128), (128, 384), (384, 512))
 LAST_PIECES = 4
 
 
@@ -50,36 +53,49 @@ def tile_picked_tokens_plain_twin_reposted_store_endcontrast_kernel(
             nc.sync.dma_start(tile[:].bitcast(I32), src_i32)
             return tile
 
-        def load_scale_rows(name, src):
+        def load_scale_rows(name, src, queue):
             width = src.shape[2] // 4
             rows = keep.tile([PACK, QUADS, width], I32, name=name)
-            nc.sync.dma_start(rows[:], src[0].bitcast(I32).rearrange("(q i) c -> i q c", i=PACK))
+            queue.dma_start(rows[:], src[0].bitcast(I32).rearrange("(q i) c -> i q c", i=PACK))
             return rows
 
-        def spread_scale_rows(name, rows):
+        def spread_scale_rows(name, rows, tag):
             width = rows[:].shape[2]
-            plane = keep.tile([P, 4 * width], U8, name=name, align_bytes=64)
+            plane = keep.tile([P, 4 * width], U8, name=name, tag=tag, align_bytes=64)
             view = plane[:].bitcast(I32)
             nc.vector.memset(view, 0)
             for q in range(QUADS):
                 nc.vector.tensor_copy(view[32 * q : 32 * q + PACK, :], rows[:, q, :])
             return plane
 
+        def load_scale_plane(name, src):
+            plane = keep.tile([P, src.shape[2]], U8, name=name, align_bytes=64)
+            view = plane[:].bitcast(I32)
+            nc.vector.memset(view, 0)
+            for q in range(QUADS):
+                nc.sync.dma_start(view[32 * q : 32 * q + PACK, :], src[0].bitcast(I32)[PACK * q : PACK * (q + 1), :])
+            return plane
+
         def fp8_words(src):
             return src[0].rearrange("p n t -> p (n t)").bitcast(I32)
 
-        def board(name, columns):
-            tile = keep.tile([P, columns], F32, name=name)
-            nc.vector.memset(tile[:], 0.0)
+        def first_board(t):
+            tile = keep.tile([P, C], F32, name="pw", bufs=EARLY)
+            (nc.vector if t < EARLY else nc.gpsimd).memset(tile[:], 0.0)
             return tile
 
-        xt_rows = load_scale_rows("xt_rows", xt_scales)
+        def board_over(tag, columns):
+            tile = keep.tile([P, columns], F32, name="over_" + tag, tag=tag, align_bytes=64)
+            nc.gpsimd.memset(tile[:], 0.0)
+            return tile
+
+        w_rows = load_scale_rows("w_rows", w_scales, nc.scalar)
         list1 = load_list("list1", offs)
-        xt_table = load_words("xt_table", xt_words[0].bitcast(I32), U16, T)
-        w_rows = load_scale_rows("w_rows", w_scales)
         w_raw = load_words("w_raw", fp8_words(w_words), I32, R)
+        xt_plane = load_scale_plane("xt_plane", xt_scales)
+        xt_table = load_words("xt_table", xt_words[0].bitcast(I32), U16, T)
         list2 = load_list("list2", offs2)
-        w2_rows = load_scale_rows("w2_rows", w2_scales)
+        w2_rows = load_scale_rows("w2_rows", w2_scales, nc.sync)
         w2_raw = load_words("w2_raw", fp8_words(w2_words), I32, R)
         list3 = load_list("list3", offs3)
         list4 = load_list("list4", offs4)
@@ -87,142 +103,179 @@ def tile_picked_tokens_plain_twin_reposted_store_endcontrast_kernel(
         nc.sync.dma_start(gain[:], sa.rearrange("(p t) o -> p (t o)", t=PACK))
         list5 = load_list("list5", offs5)
         list6 = load_list("list6", offs6)
-        vs_rows = load_scale_rows("vs_rows", vs_scales)
         vs_table = load_words("vs_table", fp8_words(vs_words), U32, Z)
+        vs_plane = load_scale_plane("vs_plane", vs_scales)
         list7 = load_list("list7", offs7)
 
-        xt_plane = spread_scale_rows("xt_plane", xt_rows)
-        token_words, token_scales = [], []
+        idle = keep.tile([P, 2], F32, name="idle")
+        nc.gpsimd.memset(idle[:, 0:1], 0.0)
+        nc.scalar.activation(idle[:, 1:2], idle[:, 0:1], ABS)
 
-        def gather_tokens(i):
-            lo, hi = SLOT_PIECES[i]
-            words = keep.tile([P, hi - lo], U16, name="token_words%d" % i, align_bytes=64)
-            scales = keep.tile([P, hi - lo], U8, name="token_scales%d" % i, align_bytes=64)
-            nc.vector.tensor_copy(scales[:], xt_plane[:].indirect(entries(list1, lo, hi)))
-            nc.vector.tensor_copy(words[:], xt_table[:].indirect(entries(list1, lo, hi)))
-            token_words.append(words)
-            token_scales.append(scales)
+        w_plane = spread_scale_rows("w_plane", w_rows, "w_plane")
+        w_dealt = keep.tile([P, PACK, P], U32, name="w_dealt", align_bytes=64)
+        w_by_tile = w_raw[:].bitcast(U32).rearrange("p (m t) -> p t m", t=PACK)
+        nc.scalar.copy(w_dealt[:, 0, :], w_by_tile[:, 0, :])
+        nc.scalar.copy(w_dealt[:, 1:, :], w_by_tile[:, 1:, :])
 
-        def deal(name, raw, plane, t):
-            words = keep.tile([P, P], I32, name="%s_words%d" % (name, t), align_bytes=64)
-            scales = keep.tile([P, P], U8, name="%s_scales%d" % (name, t), align_bytes=64)
+        def deal_scales(tag, bufs, plane, t):
+            scales = keep.tile([P, P], U8, name="dealt_scales", tag=tag, bufs=bufs, align_bytes=64)
             nc.vector.tensor_copy(scales[:], plane[:, t::PACK])
-            nc.vector.tensor_copy(words[:], raw[:, t::PACK])
-            return words, scales
+            return scales[:]
 
-        def multiply_tokens(acc, weights, i):
+        def first_weights(t):
+            return w_dealt[:, t, :], deal_scales("w_scales", EARLY, w_plane, t)
+
+        def second_weights(t):
+            words = keep.tile([P, P], I32, name="w2_words%d" % t, align_bytes=64)
+            nc.vector.tensor_copy(words[:], w2_raw[:, t::PACK])
+            return words[:], deal_scales("w2_scales%d" % t, 1, w2_plane, t)
+
+        token_words = keep.tile([P, J], U16, name="token_words", align_bytes=64)
+        head_scales = keep.tile([P, HEAD], U8, name="head_scales", align_bytes=64)
+        rest_scales = keep.tile([P, J - HEAD], U8, name="rest_scales", tag="xt_table", align_bytes=64)
+        early_weights = [first_weights(0)]
+        nc.vector.tensor_copy(head_scales[:], xt_plane[:].indirect(entries(list1, 0, HEAD)))
+        nc.vector.tensor_copy(token_words[:, 0:HEAD], xt_table[:].indirect(entries(list1, 0, HEAD)))
+        early_weights.extend(first_weights(t) for t in range(1, EARLY))
+        nc.vector.tensor_copy(token_words[:, HEAD:J], xt_table[:].indirect(entries(list1, HEAD, J)))
+        nc.vector.tensor_copy(rest_scales[:], xt_plane[:].indirect(entries(list1, HEAD, J)))
+
+        def multiply_tokens(acc, weights, lo, hi):
+            scales = head_scales[:] if lo == 0 else rest_scales[:]
             nc.tensor.matmul_mx(
-                out=acc, lhsT=weights[0][:].bitcast(FP8X4), lhsT_scale=weights[1][:],
-                rhs=token_words[i][:].bitcast(FP4X4), rhs_scale=token_scales[i][:], start=True, stop=True,
+                out=acc, lhsT=weights[0].bitcast(FP8X4), lhsT_scale=weights[1],
+                rhs=token_words[:, lo:hi].bitcast(FP4X4), rhs_scale=scales, start=True, stop=True,
             )
 
         def product(name, weights):
             acc = psum.tile([P, 512], F32, name="bank")
-            for i, (lo, hi) in enumerate(SLOT_PIECES):
-                multiply_tokens(acc[:, lo:hi], weights, i)
-            result = keep.tile([P, J], F32, name=name)
+            for lo, hi in SLOT_PIECES:
+                multiply_tokens(acc[:, lo:hi], weights, lo, hi)
+            result = keep.tile([P, J], F32, name=name, align_bytes=64)
             nc.vector.tensor_copy(result[:], acc[:, 0:J])
             return result
 
-        pw = [board("pw0", C)]
-        gather_tokens(0)
-        w_plane = spread_scale_rows("w_plane", w_rows)
-        first_weights = deal("w", w_raw, w_plane, 0)
-        first = keep.tile([P, J], F32, name="a0")
-        for i, (lo, hi) in enumerate(SLOT_PIECES):
-            if i > 0:
-                gather_tokens(i)
-            acc = psum.tile([P, 512], F32, name="bank")
-            multiply_tokens(acc[:, 0 : hi - lo], first_weights, i)
-            nc.vector.tensor_copy(first[:, lo:hi], acc[:, 0 : hi - lo])
-        w2_plane = spread_scale_rows("w2_plane", w2_rows)
-        a, b, pv, pu = [first], [], [], []
+        a = [keep.tile([P, J], F32, name="a%d" % t, align_bytes=64) for t in range(EARLY)]
+        for lo, hi in SLOT_PIECES:
+            for t in range(EARLY):
+                acc = psum.tile([P, 512], F32, name="bank")
+                multiply_tokens(acc[:, 0 : hi - lo], early_weights[t], lo, hi)
+                leave = nc.scalar.copy if lo == 0 else nc.vector.tensor_copy
+                leave(a[t][:, lo:hi], acc[:, 0 : hi - lo])
+        b = []
         for t in range(PACK):
-            if t > 0:
-                pw.append(board("pw%d" % t, C))
-                a.append(product("a%d" % t, deal("w", w_raw, w_plane, t)))
-            pv.append(board("pv%d" % t, C))
-            b.append(product("b%d" % t, deal("w2", w2_raw, w2_plane, t)))
-            pu.append(board("pu%d" % t, C))
+            if EARLY <= t + 1 < PACK:
+                a.append(product("a%d" % (t + 1), first_weights(t + 1)))
+            if t == 0:
+                w2_plane = spread_scale_rows("w2_plane", w2_rows, "xt_plane")
+            b.append(product("b%d" % t, second_weights(t)))
 
-        vs_plane = spread_scale_rows("vs_plane", vs_rows)
-        store_words = keep.tile([P, N], U32, name="store_words", align_bytes=64)
-        store_scales = keep.tile([P, N], U8, name="store_scales", align_bytes=64)
+        store_words = keep.tile([P, N], U32, name="store_words", tag="token_words", align_bytes=64)
+        store_scales = keep.tile([P, N], U8, name="store_scales", tag="head_scales", align_bytes=64)
         nc.vector.tensor_copy(store_scales[:], vs_plane[:].indirect(list6[:]))
         nc.vector.tensor_copy(store_words[:], vs_table[:].indirect(list6[:]))
-        pages = [board("page%d" % nt, U) for nt in range(N // P)]
+        pages = [board_over(tag, U) for tag in ("w2_raw", "vs_table")]
 
         def scatter(window, offsets, values):
             nc.scalar.activation(window[:].indirect(offsets), values, COPY)
 
-        picked = [keep.tile([P, S], F32, name="picked%d" % t) for t in range(PACK)]
+        picked = [
+            keep.tile([P, S], F32, name="picked%d" % t, tag="w2_words%d" % t, align_bytes=64)
+            for t in range(PACK)
+        ]
 
         def pick(t):
             nc.scalar.activation(picked[t][:], pw[t][:].indirect(list4[:]), COPY, scale=gain[:, t : t + 1])
 
-        for lo, hi in SLOT_PIECES:
-            scatter(pw[0], entries(list2, lo, hi), a[0][:, lo:hi])
-        for t in range(PACK):
-            if t + 1 < PACK:
-                scatter(pv[t], list3[:], b[t][:])
-                pick(t)
-                scatter(pw[t + 1], list2[:], a[t + 1][:])
-            else:
-                pick(t)
-                scatter(pv[t], list3[:], b[t][:])
-            scatter(pu[t], list5[:], picked[t][:])
-
         hid = keep.tile([P, C, PACK], BF16, name="hid", align_bytes=64)
-        diff = [keep.tile([P, C], F32, name="diff%d" % t) for t in range(PACK)]
 
-        def contrast(t, lo, hi):
-            nc.vector.tensor_tensor(diff[t][:, lo:hi], pv[t][:, lo:hi], pu[t][:, lo:hi], ALU.subtract)
-            nc.vector.scalar_tensor_tensor(
-                hid[:, lo:hi, t], diff[t][:, lo:hi], -1.0, diff[t][:, lo:hi], ALU.mult, ALU.max
-            )
+        def difference(t, pieces):
+            diff = keep.tile([P, C], F32, name="diff")
+            for lo, hi in pieces:
+                nc.vector.tensor_tensor(diff[:, lo:hi], pv[t][:, lo:hi], pu[t][:, lo:hi], ALU.subtract)
+            return diff
 
-        for t in range(PACK - 1):
-            contrast(t, 0, C)
+        def magnitude_on_vector(t, lo, hi, diff):
+            nc.vector.scalar_tensor_tensor(hid[:, lo:hi, t], diff[:, lo:hi], -1.0, diff[:, lo:hi], ALU.mult, ALU.max)
+
+        def magnitude_on_scalar(t, lo, hi, diff):
+            nc.scalar.activation(hid[:, lo:hi, t], diff[:, lo:hi], ABS)
+
+        pw, pv, pu = [first_board(t) for t in range(EARLY)], [], []
+        for lo, hi in SLOT_PIECES:
+            for t in range(EARLY):
+                scatter(pw[t], entries(list2, lo, hi), a[t][:, lo:hi])
+        for t in range(PACK):
+            if EARLY <= t + 1 < PACK:
+                pw.append(first_board(t + 1))
+                scatter(pw[t + 1], list2[:], a[t + 1][:])
+            pick(t)
+            pv.append(board_over("a%d" % t, C))
+            scatter(pv[t], list3[:], b[t][:])
+            pu.append(board_over("w2_scales%d" % t, C))
+            scatter(pu[t], list5[:], picked[t][:])
+            if t + 1 < PACK:
+                magnitude_on_vector(t, 0, C, difference(t, ((0, C),)))
 
         results = [keep.tile([P, C], F32, name="result%d" % nt) for nt in range(N // P)]
-        for i, (lo, hi) in enumerate(COLUMN_PIECES):
-            contrast(PACK - 1, lo, hi)
-            codes = keep.tile([P, hi - lo], U32, name="hid_words%d" % i, align_bytes=64)
-            scales = keep.tile([P, hi - lo], U8, name="hid_scales%d" % i, align_bytes=64)
+        last_diff = difference(PACK - 1, COLUMN_PIECES)
+        for lo, hi in COLUMN_PIECES[:-1]:
+            magnitude_on_scalar(PACK - 1, lo, hi, last_diff)
+        def quantise(lo, hi):
+            words = keep.tile([P, hi - lo], U32, name="hid_words%d" % lo, align_bytes=64)
+            scales = keep.tile([P, hi - lo], U8, name="hid_scales%d" % lo, align_bytes=64)
             nc.vector.quantize_mx(
-                out=codes[:].bitcast(FP8X4), scales=scales[:],
+                out=words[:].bitcast(FP8X4), scales=scales[:],
                 in_=hid[:, lo:hi, :].rearrange("p c t -> p (c t)"),
             )
+            return words, scales
+
+        def multiply_store(nt, lo, hi, quantised):
+            acc = psum.tile([P, 512], F32, name="bank")
+            nc.tensor.matmul_mx(
+                out=acc[:, 0 : hi - lo],
+                lhsT=store_words[:, nt * P : (nt + 1) * P].bitcast(FP8X4),
+                lhsT_scale=store_scales[:, nt * P : (nt + 1) * P],
+                rhs=quantised[0][:].bitcast(FP8X4), rhs_scale=quantised[1][:], start=True, stop=True,
+            )
+            nc.vector.tensor_copy(results[nt][:, lo:hi], acc[:, 0 : hi - lo])
+
+        for lo, hi in COLUMN_PIECES[:2]:
+            quantised = quantise(lo, hi)
             for nt in range(N // P):
-                acc = psum.tile([P, 512], F32, name="bank")
-                nc.tensor.matmul_mx(
-                    out=acc[:, 0 : hi - lo],
-                    lhsT=store_words[:, nt * P : (nt + 1) * P].bitcast(FP8X4),
-                    lhsT_scale=store_scales[:, nt * P : (nt + 1) * P],
-                    rhs=codes[:].bitcast(FP8X4), rhs_scale=scales[:], start=True, stop=True,
-                )
-                nc.vector.tensor_copy(results[nt][:, lo:hi], acc[:, 0 : hi - lo])
+                multiply_store(nt, lo, hi, quantised)
+        magnitude_on_vector(PACK - 1, *COLUMN_PIECES[-1], last_diff)
+        wide = [quantise(lo, hi) for lo, hi in COLUMN_PIECES[2:]]
+        for nt in range(N // P):
+            for (lo, hi), quantised in zip(COLUMN_PIECES[2:], wide):
+                multiply_store(nt, lo, hi, quantised)
 
         def post(nt, lo, hi):
             scatter(pages[nt], entries(list7, lo, hi), results[nt][:, lo:hi])
 
-        post(0, *COLUMN_PIECES[0])
-        post(1, *COLUMN_PIECES[0])
-        for lo, hi in COLUMN_PIECES[1:]:
-            post(0, lo, hi)
-        post(1, COLUMN_PIECES[1][0], C)
+        for lo, hi in COLUMN_PIECES[:2] + ((COLUMN_PIECES[2][0], C),):
+            for nt in range(N // P):
+                post(nt, lo, hi)
 
         for nt in range(N // P):
-            width = U // LAST_PIECES
-            sums = keep.tile([P, E], F32, name="sums%d" % nt)
-            final = keep.tile([P, U], F32, name="final%d" % nt)
-            for lo in range(0, U, width):
-                page = pages[nt][:, lo : lo + width].rearrange("p (e j) -> p e j", j=BUCKET)
-                total = sums[:, lo // BUCKET : (lo + width) // BUCKET]
-                nc.vector.tensor_reduce(total, page, AXIS_X, ALU.add)
+            page = pages[nt][:].rearrange("p (e j) -> p e j", j=BUCKET)
+            partial = keep.tile([P, 3 * E], F32, name="partial")
+            pairs = partial[:, 0 : 2 * E].rearrange("p (e j) -> p e j", j=2)
+            sums = partial[:, 2 * E : 3 * E]
+            final = keep.tile([P, E, BUCKET], F32, name="final%d" % nt)
+            halves = [slice(lo, lo + E // 2) for lo in range(0, E, E // 2)]
+            for e in halves:
+                nc.vector.tensor_tensor(pairs[:, e, :], page[:, e, 0:2], page[:, e, 2:4], ALU.add)
+            for e in halves:
+                nc.vector.tensor_tensor(sums[:, e], pairs[:, e, 0], pairs[:, e, 1], ALU.add)
+            width = E // LAST_PIECES
+            for lo in range(0, E, width):
+                e = slice(lo, lo + width)
                 nc.vector.scalar_tensor_tensor(
-                    final[:, lo : lo + width].rearrange("p (e j) -> p e j", j=BUCKET),
-                    total.unsqueeze(2).to_broadcast([P, width // BUCKET, BUCKET]),
-                    -1.0 / BUCKET, page, ALU.mult, ALU.add,
+                    final[:, e, :], sums[:, e].unsqueeze(2).to_broadcast([P, width, BUCKET]),
+                    -1.0 / BUCKET, page[:, e, :], ALU.mult, ALU.add,
                 )
-                nc.sync.dma_start(out[nt * P : (nt + 1) * P, lo : lo + width], final[:, lo : lo + width])
+                nc.sync.dma_start(
+                    out[nt * P : (nt + 1) * P, BUCKET * lo : BUCKET * (lo + width)],
+                    final[:, e, :].rearrange("p e j -> p (e j)"),
+                )

from contextlib import ExitStack

import concourse.mybir as mybir

F32 = mybir.dt.float32
BF16 = mybir.dt.bfloat16
I32 = mybir.dt.int32
U32 = mybir.dt.uint32
U16 = mybir.dt.uint16
U8 = mybir.dt.uint8
FP8X4 = mybir.dt.float8_e4m3fn_x4
FP4X4 = mybir.dt.float4_e2m1fn_x4
ALU = mybir.AluOpType
COPY = mybir.ActivationFunctionType.Copy
ABS = mybir.ActivationFunctionType.Abs
AXIS_X = mybir.AxisListType.X

K, J, R, T, C, S, N, Z, U, E = 512, 384, 512, 1024, 512, 128, 256, 1024, 1024, 256
FLOPS = 2 * (2 * K * R * J + R * N * C)

P = 128
PACK = 4
QUADS = 4
LANES = 16
BUCKET = U // E
HEAD = 128
EARLY = 2
SLOT_PIECES = ((0, HEAD), (HEAD, J))
COLUMN_PIECES = ((0, 64), (64, 128), (128, 384), (384, 512))
LAST_PIECES = 4


def entries(offsets, lo, hi):
    return offsets[:, lo // LANES : hi // LANES]


def tile_picked_tokens_plain_twin_reposted_store_endcontrast_kernel(
    tc, xt_words, xt_scales, w_words, w_scales, w2_words, w2_scales, sa, vs_words, vs_scales,
    offs, offs2, offs3, offs4, offs5, offs6, offs7, out,
):
    nc = tc.nc
    with ExitStack() as ctx:
        keep = ctx.enter_context(tc.tile_pool(name="keep", bufs=1))
        psum = ctx.enter_context(tc.psum_pool(name="psum", bufs=8))

        def load_list(name, src):
            tile = keep.tile(list(src.shape), U16, name=name)
            nc.sync.dma_start(tile[:], src)
            return tile

        def load_words(name, src_i32, dtype, columns):
            tile = keep.tile([P, columns], dtype, name=name, align_bytes=64)
            nc.sync.dma_start(tile[:].bitcast(I32), src_i32)
            return tile

        def load_scale_rows(name, src, queue):
            width = src.shape[2] // 4
            rows = keep.tile([PACK, QUADS, width], I32, name=name)
            queue.dma_start(rows[:], src[0].bitcast(I32).rearrange("(q i) c -> i q c", i=PACK))
            return rows

        def spread_scale_rows(name, rows, tag):
            width = rows[:].shape[2]
            plane = keep.tile([P, 4 * width], U8, name=name, tag=tag, align_bytes=64)
            view = plane[:].bitcast(I32)
            nc.vector.memset(view, 0)
            for q in range(QUADS):
                nc.vector.tensor_copy(view[32 * q : 32 * q + PACK, :], rows[:, q, :])
            return plane

        def load_scale_plane(name, src):
            plane = keep.tile([P, src.shape[2]], U8, name=name, align_bytes=64)
            view = plane[:].bitcast(I32)
            nc.vector.memset(view, 0)
            for q in range(QUADS):
                nc.sync.dma_start(view[32 * q : 32 * q + PACK, :], src[0].bitcast(I32)[PACK * q : PACK * (q + 1), :])
            return plane

        def fp8_words(src):
            return src[0].rearrange("p n t -> p (n t)").bitcast(I32)

        def first_board(t):
            tile = keep.tile([P, C], F32, name="pw", bufs=EARLY)
            (nc.vector if t < EARLY else nc.gpsimd).memset(tile[:], 0.0)
            return tile

        def board_over(tag, columns):
            tile = keep.tile([P, columns], F32, name="over_" + tag, tag=tag, align_bytes=64)
            nc.gpsimd.memset(tile[:], 0.0)
            return tile

        w_rows = load_scale_rows("w_rows", w_scales, nc.scalar)
        list1 = load_list("list1", offs)
        w_raw = load_words("w_raw", fp8_words(w_words), I32, R)
        xt_plane = load_scale_plane("xt_plane", xt_scales)
        xt_table = load_words("xt_table", xt_words[0].bitcast(I32), U16, T)
        list2 = load_list("list2", offs2)
        w2_rows = load_scale_rows("w2_rows", w2_scales, nc.sync)
        w2_raw = load_words("w2_raw", fp8_words(w2_words), I32, R)
        list3 = load_list("list3", offs3)
        list4 = load_list("list4", offs4)
        gain = keep.tile([P, PACK], F32, name="gain")
        nc.sync.dma_start(gain[:], sa.rearrange("(p t) o -> p (t o)", t=PACK))
        list5 = load_list("list5", offs5)
        list6 = load_list("list6", offs6)
        vs_table = load_words("vs_table", fp8_words(vs_words), U32, Z)
        vs_plane = load_scale_plane("vs_plane", vs_scales)
        list7 = load_list("list7", offs7)

        idle = keep.tile([P, 2], F32, name="idle")
        nc.gpsimd.memset(idle[:, 0:1], 0.0)
        nc.scalar.activation(idle[:, 1:2], idle[:, 0:1], ABS)

        w_plane = spread_scale_rows("w_plane", w_rows, "w_plane")
        w_dealt = keep.tile([P, PACK, P], U32, name="w_dealt", align_bytes=64)
        w_by_tile = w_raw[:].bitcast(U32).rearrange("p (m t) -> p t m", t=PACK)
        nc.scalar.copy(w_dealt[:, 0, :], w_by_tile[:, 0, :])
        nc.scalar.copy(w_dealt[:, 1:, :], w_by_tile[:, 1:, :])

        def deal_scales(tag, bufs, plane, t):
            scales = keep.tile([P, P], U8, name="dealt_scales", tag=tag, bufs=bufs, align_bytes=64)
            nc.vector.tensor_copy(scales[:], plane[:, t::PACK])
            return scales[:]

        def first_weights(t):
            return w_dealt[:, t, :], deal_scales("w_scales", EARLY, w_plane, t)

        def second_weights(t):
            words = keep.tile([P, P], I32, name="w2_words%d" % t, align_bytes=64)
            nc.vector.tensor_copy(words[:], w2_raw[:, t::PACK])
            return words[:], deal_scales("w2_scales%d" % t, 1, w2_plane, t)

        token_words = keep.tile([P, J], U16, name="token_words", align_bytes=64)
        head_scales = keep.tile([P, HEAD], U8, name="head_scales", align_bytes=64)
        rest_scales = keep.tile([P, J - HEAD], U8, name="rest_scales", tag="xt_table", align_bytes=64)
        early_weights = [first_weights(0)]
        nc.vector.tensor_copy(head_scales[:], xt_plane[:].indirect(entries(list1, 0, HEAD)))
        nc.vector.tensor_copy(token_words[:, 0:HEAD], xt_table[:].indirect(entries(list1, 0, HEAD)))
        early_weights.extend(first_weights(t) for t in range(1, EARLY))
        nc.vector.tensor_copy(token_words[:, HEAD:J], xt_table[:].indirect(entries(list1, HEAD, J)))
        nc.vector.tensor_copy(rest_scales[:], xt_plane[:].indirect(entries(list1, HEAD, J)))

        def multiply_tokens(acc, weights, lo, hi):
            scales = head_scales[:] if lo == 0 else rest_scales[:]
            nc.tensor.matmul_mx(
                out=acc, lhsT=weights[0].bitcast(FP8X4), lhsT_scale=weights[1],
                rhs=token_words[:, lo:hi].bitcast(FP4X4), rhs_scale=scales, start=True, stop=True,
            )

        def product(name, weights):
            acc = psum.tile([P, 512], F32, name="bank")
            for lo, hi in SLOT_PIECES:
                multiply_tokens(acc[:, lo:hi], weights, lo, hi)
            result = keep.tile([P, J], F32, name=name, align_bytes=64)
            nc.vector.tensor_copy(result[:], acc[:, 0:J])
            return result

        a = [keep.tile([P, J], F32, name="a%d" % t, align_bytes=64) for t in range(EARLY)]
        for lo, hi in SLOT_PIECES:
            for t in range(EARLY):
                acc = psum.tile([P, 512], F32, name="bank")
                multiply_tokens(acc[:, 0 : hi - lo], early_weights[t], lo, hi)
                leave = nc.scalar.copy if lo == 0 else nc.vector.tensor_copy
                leave(a[t][:, lo:hi], acc[:, 0 : hi - lo])
        b = []
        for t in range(PACK):
            if EARLY <= t + 1 < PACK:
                a.append(product("a%d" % (t + 1), first_weights(t + 1)))
            if t == 0:
                w2_plane = spread_scale_rows("w2_plane", w2_rows, "xt_plane")
            b.append(product("b%d" % t, second_weights(t)))

        store_words = keep.tile([P, N], U32, name="store_words", tag="token_words", align_bytes=64)
        store_scales = keep.tile([P, N], U8, name="store_scales", tag="head_scales", align_bytes=64)
        nc.vector.tensor_copy(store_scales[:], vs_plane[:].indirect(list6[:]))
        nc.vector.tensor_copy(store_words[:], vs_table[:].indirect(list6[:]))
        pages = [board_over(tag, U) for tag in ("w2_raw", "vs_table")]

        def scatter(window, offsets, values):
            nc.scalar.activation(window[:].indirect(offsets), values, COPY)

        picked = [
            keep.tile([P, S], F32, name="picked%d" % t, tag="w2_words%d" % t, align_bytes=64)
            for t in range(PACK)
        ]

        def pick(t):
            nc.scalar.activation(picked[t][:], pw[t][:].indirect(list4[:]), COPY, scale=gain[:, t : t + 1])

        hid = keep.tile([P, C, PACK], BF16, name="hid", align_bytes=64)

        def difference(t, pieces):
            diff = keep.tile([P, C], F32, name="diff")
            for lo, hi in pieces:
                nc.vector.tensor_tensor(diff[:, lo:hi], pv[t][:, lo:hi], pu[t][:, lo:hi], ALU.subtract)
            return diff

        def magnitude_on_vector(t, lo, hi, diff):
            nc.vector.scalar_tensor_tensor(hid[:, lo:hi, t], diff[:, lo:hi], -1.0, diff[:, lo:hi], ALU.mult, ALU.max)

        def magnitude_on_scalar(t, lo, hi, diff):
            nc.scalar.activation(hid[:, lo:hi, t], diff[:, lo:hi], ABS)

        pw, pv, pu = [first_board(t) for t in range(EARLY)], [], []
        for lo, hi in SLOT_PIECES:
            for t in range(EARLY):
                scatter(pw[t], entries(list2, lo, hi), a[t][:, lo:hi])
        for t in range(PACK):
            if EARLY <= t + 1 < PACK:
                pw.append(first_board(t + 1))
                scatter(pw[t + 1], list2[:], a[t + 1][:])
            pick(t)
            pv.append(board_over("a%d" % t, C))
            scatter(pv[t], list3[:], b[t][:])
            pu.append(board_over("w2_scales%d" % t, C))
            scatter(pu[t], list5[:], picked[t][:])
            if t + 1 < PACK:
                magnitude_on_vector(t, 0, C, difference(t, ((0, C),)))

        results = [keep.tile([P, C], F32, name="result%d" % nt) for nt in range(N // P)]
        last_diff = difference(PACK - 1, COLUMN_PIECES)
        for lo, hi in COLUMN_PIECES[:-1]:
            magnitude_on_scalar(PACK - 1, lo, hi, last_diff)
        def quantise(lo, hi):
            words = keep.tile([P, hi - lo], U32, name="hid_words%d" % lo, align_bytes=64)
            scales = keep.tile([P, hi - lo], U8, name="hid_scales%d" % lo, align_bytes=64)
            nc.vector.quantize_mx(
                out=words[:].bitcast(FP8X4), scales=scales[:],
                in_=hid[:, lo:hi, :].rearrange("p c t -> p (c t)"),
            )
            return words, scales

        def multiply_store(nt, lo, hi, quantised):
            acc = psum.tile([P, 512], F32, name="bank")
            nc.tensor.matmul_mx(
                out=acc[:, 0 : hi - lo],
                lhsT=store_words[:, nt * P : (nt + 1) * P].bitcast(FP8X4),
                lhsT_scale=store_scales[:, nt * P : (nt + 1) * P],
                rhs=quantised[0][:].bitcast(FP8X4), rhs_scale=quantised[1][:], start=True, stop=True,
            )
            nc.vector.tensor_copy(results[nt][:, lo:hi], acc[:, 0 : hi - lo])

        for lo, hi in COLUMN_PIECES[:2]:
            quantised = quantise(lo, hi)
            for nt in range(N // P):
                multiply_store(nt, lo, hi, quantised)
        magnitude_on_vector(PACK - 1, *COLUMN_PIECES[-1], last_diff)
        wide = [quantise(lo, hi) for lo, hi in COLUMN_PIECES[2:]]
        for nt in range(N // P):
            for (lo, hi), quantised in zip(COLUMN_PIECES[2:], wide):
                multiply_store(nt, lo, hi, quantised)

        def post(nt, lo, hi):
            scatter(pages[nt], entries(list7, lo, hi), results[nt][:, lo:hi])

        for lo, hi in COLUMN_PIECES[:2] + ((COLUMN_PIECES[2][0], C),):
            for nt in range(N // P):
                post(nt, lo, hi)

        for nt in range(N // P):
            page = pages[nt][:].rearrange("p (e j) -> p e j", j=BUCKET)
            partial = keep.tile([P, 3 * E], F32, name="partial")
            pairs = partial[:, 0 : 2 * E].rearrange("p (e j) -> p e j", j=2)
            sums = partial[:, 2 * E : 3 * E]
            final = keep.tile([P, E, BUCKET], F32, name="final%d" % nt)
            halves = [slice(lo, lo + E // 2) for lo in range(0, E, E // 2)]
            for e in halves:
                nc.vector.tensor_tensor(pairs[:, e, :], page[:, e, 0:2], page[:, e, 2:4], ALU.add)
            for e in halves:
                nc.vector.tensor_tensor(sums[:, e], pairs[:, e, 0], pairs[:, e, 1], ALU.add)
            width = E // LAST_PIECES
            for lo in range(0, E, width):
                e = slice(lo, lo + width)
                nc.vector.scalar_tensor_tensor(
                    final[:, e, :], sums[:, e].unsqueeze(2).to_broadcast([P, width, BUCKET]),
                    -1.0 / BUCKET, page[:, e, :], ALU.mult, ALU.add,
                )
                nc.sync.dma_start(
                    out[nt * P : (nt + 1) * P, BUCKET * lo : BUCKET * (lo + width)],
                    final[:, e, :].rearrange("p e j -> p (e j)"),
                )
